import numpy as np, ml_dtypes
CORES = [5,29,101,125,133,157,229,253]
N = 8
import mx_ref
BF = ml_dtypes.bfloat16
def gentries(a):
    return np.ascontiguousarray(a.reshape(8, 16, -1).transpose(0, 2, 1)).reshape(8, -1)
def gtable(e):
    e = np.asarray(e); return np.ascontiguousarray(e.reshape(8, -1, 16).transpose(0, 2, 1)).reshape(128, -1).astype(np.int32)
def gcols(t, e):
    v = np.concatenate([t.reshape(8, 16, -1, 4), np.zeros((8, 16, 1, 4), BF)], axis=2)
    return np.ascontiguousarray(np.stack([v[g][:, e[g]] for g in range(8)])).reshape(128, -1)
def tile(rs):
    return np.stack(rs, axis=2).reshape(128, -1).astype(BF)
def pick(q, e):
    c = np.concatenate([q[0].reshape(128, -1, 4), np.zeros((128, 1, 4), np.uint8)], axis=1); s = np.concatenate([q[1], np.ones((16, 1), np.uint8)], axis=1)
    return (np.ascontiguousarray(c[:, e].reshape(128, -1)), np.ascontiguousarray(s[:, e]))
def join(*qs):
    return (np.concatenate([q[0] for q in qs], axis=1), np.concatenate([q[1] for q in qs], axis=1))
def put(q, e, v):
    c, s = q[0].reshape(128, -1, 4).copy(), q[1].copy(); c[:, e] = v[0].reshape(128, -1, 4); s[:, e] = v[1]
    return (c.reshape(128, -1), s)
def pk(c, s):
    return (np.ascontiguousarray(c), mx_ref.live(s))
def emit(q):
    return q[0], q[1]
def packed(v, rng):
    q = [mx_ref.quantize(np.ascontiguousarray(v[r])) for r in range(N)]
    return np.stack([a for a, b in q]), np.stack([mx_ref.plane(b, rng) for a, b in q])
def values_of_codes():
    e, c = np.zeros((128, 128, 4), np.float32), np.zeros((128, 2, 4), np.uint8)
    e[np.arange(128), np.arange(128), 0] = 1
    c[:127, :, 0] = np.arange(256).reshape(2, 128).T[:127]
    return mx_ref.matmul(mx_ref.quantize(e.reshape(128, 512).astype(BF)), (c.reshape(128, 8), np.full((16, 2), 127, np.uint8))).T.reshape(-1).astype(np.float64)
CODE_VALUE, SCALE_VALUE = values_of_codes(), 2.0 ** (np.arange(256) - 127.0)
def decode(q):
    return (CODE_VALUE[q[0]].reshape(16, 8, -1, 4) * SCALE_VALUE[q[1]][:, None, :, None] + 0.0).reshape(128, -1).astype(np.float32)
def f(rng, *shape):
    return mx_ref.flush((rng.standard_normal(shape, dtype=np.float32) * np.exp2(rng.integers(-2, 3, shape[:-1] + (1,)))).astype(BF))
def wide(rng, *shape, cols=0):
    v = rng.standard_normal(shape, dtype=np.float32) * np.exp2(rng.integers(-12, 13, shape)).astype(np.float32)
    if cols: v *= np.repeat(np.exp2(rng.integers(-cols, cols + 1, shape[:-2] + (1, shape[-1] // 4))) * (rng.random(shape[:-2] + (1, shape[-1] // 4)) > 0.0625), 4, axis=-1).astype(np.float32)
    return mx_ref.flush(v.astype(BF))
C, K = 320, 80
STRIDE = [1, 2, 4]
def at(t, e):
    return np.take_along_axis(t, e, axis=1)
def halved(a, b):
    return ((a.astype(np.float32) + b.astype(np.float32)) * np.float32(0.5)).astype(BF)
def big(v):
    v = np.array(v).astype(np.float32)
    v[np.abs(v) < np.float32(2.0 ** -16)] = 0
    return np.clip(v, -2.0 ** 21, 2.0 ** 21).astype(BF)
def numbers_of(rng):
    return {"x": big(f(rng, N, 128, 4 * C)), "u": np.array(f(rng, N, 128, 512)), "v": np.array(f(rng, N, 128, 512))}
def pairs(a, b):
    e = np.zeros(C, np.int64)
    e[a] = b
    e[b] = a
    return e
def pairing(rng):
    z = rng.permutation(C).reshape(2, -1)
    return pairs(z[0], z[1])
def pairings(rng):
    return np.stack([gtable(np.stack([pairing(rng) for g in range(8)])) for r in range(N)])
def layers(rng, still=[]):
    w = big(f(rng, N, 128, 2048).astype(np.float32) * np.float32(0.0625)).reshape(N, 8, 16, 4, 8, 16, 4)
    for i in still:
        w[:, :, i] = 0
        w[:, :, :, :, :, i] = 0
    return w
def weights(rng, w):
    c, s = packed(np.ascontiguousarray(w).reshape(N, 128, 2048), rng)
    return {"wc": c, "ws": s}
def setup_inputs(rng):
    return {**numbers_of(rng), "m": pairings(rng), **weights(rng, layers(rng))}
def setup_inputs_ties(rng):
    d = numbers_of(rng)
    x = d["x"].reshape(N, 8, 16, C, 4)
    x[:, :, 0] = 0
    x[:, :, 0, :, 0] = rng.integers(1, 4, (N, 8, C)).astype(np.float32).astype(BF)
    u = d["u"].reshape(N, 128, 128, 4)
    u[:, :, ::16] = 0
    o = rng.permutation(N)
    for r in range(N):
        for h in range(0, 128, 16): u[r, h, h, 0] = 0.0 if r == o[0] else -1.0 if r == o[1] else 1.0
    w = layers(rng, [0])
    a = 2 * int(rng.integers(N // 2))
    x[a, :, 8:] = 2.0 ** 18
    x[a + 1, :, 8:] = -2.0 ** 18
    w[a:a + 2, :, 8:] = 0
    return {"x": x.reshape(N, 128, 4 * C), "u": u.reshape(N, 128, 512), "v": d["v"], "m": pairings(rng), **weights(rng, w)}
def setup_inputs_near(rng):
    d = numbers_of(rng)
    x = d["x"].astype(np.float32).reshape(N, 8, 16, C, 4)
    x[:, :, 0] = 0
    x[:, :, 8:] = 0
    u = d["u"].reshape(N, 128, 128, 4)
    u[:, :, ::16] = 0
    s = rng.integers(0, 16, (N, 8, C))
    digits = ((s[:, :, :, None] >> np.arange(4)) & 1) * np.exp2(np.arange(4) - 23.0)
    o = rng.permutation(N) % 4
    for r in range(N):
        sign = rng.permutation(8) % 2 * 2.0 - 1.0
        k = 2.0 ** -4 if o[r] == 1 else 1.0
        c = 1.0 if o[r] == 0 else 2.0 ** -30
        if o[r] < 2:
            x[r, :, 0, :, 0] = k
            x[r, :, 11, :, 0] = k * 2.0 ** -10
        if o[r] < 3: x[r, :, 8] = k * digits[r]
        if o[r] == 2:
            for g in rng.permutation(8)[:4]:
                a = rng.permutation(C)
                x[r, g, 0, a[0], 0] = 2.0 ** 21
                x[r, g, 0, a[1], 0] = -2.0 ** 21
        if o[r] == 3:
            e = rng.integers(0, 2, (8, C))
            x[r, :, 9, :, 0] = e * 1.125 * 2.0 ** -27
            x[r, :, 10, :, 0] = (1 - e) * 2.0 ** -27
            x[r, :, 12, :, 0] = 2.0 ** -27
        for g in range(8):
            h = 16 * g
            if o[r] < 3:
                u[r, h, h, 0] = sign[g] * (c if o[r] < 2 else 2.0 ** 30)
                u[r, h + 8, h] = sign[g] * c
            if o[r] < 2: u[r, h + 11, h, 0] = sign[g] * c
            if o[r] == 3:
                u[r, h + 9, h, 0] = sign[g] * 1.125 * c
                u[r, h + 10, h, 0] = sign[g] * 1.25 * c
                u[r, h + 12, h, 0] = sign[g] * -1.125 * c
    return {"x": x.reshape(N, 128, 4 * C).astype(BF), "u": u.reshape(N, 128, 512), "v": d["v"], "m": pairings(rng), **weights(rng, layers(rng, [0, 8, 9, 10, 11, 12, 13, 14, 15]))}
def setup_inputs_blocks(rng):
    d = numbers_of(rng)
    k = rng.integers(-2, 3, (8, 1, 1, 1, 1))
    unit = np.exp2(k * 1.0).reshape(8, 1, 1, 1)
    e = np.arange(32).reshape(8, 1, 4)
    x = np.exp2(k - rng.integers(8, 15, (N, 8, 2, 8, C, 4))) * (1.0 + (2 * rng.integers(0, 64, (N, 8, 2, 8, C, 4)) + 1) * 2.0 ** -7)
    x[:, :, 0, 1, :, 0] = np.exp2(k.reshape(8, 1) - rng.integers(13, 15, (N, 8, C))) * (1.0 + (2 * rng.integers(0, 64, (N, 8, C)) + 1) * 2.0 ** -7)
    i = rng.integers(0, 31, (N, 8, 1, C, 1))
    i = np.where(i >= 4, i + 1, i)
    x[:, :, 0] = np.where(e == i, 1.96875 * unit, x[:, :, 0])
    x = x * (rng.integers(0, 2, x.shape) * 2.0 - 1.0)
    i = rng.integers(0, 32, (N, 8, 1, 1, 1))
    x[:, :, 1] = np.where(e == i, np.where(rng.random((N, 8, 1, C, 1)) < 0.5, 3.0, 0.9375) * unit, x[:, :, 1])
    m = np.stack([np.stack([pairing(rng) for g in range(8)]) for r in range(N)])
    for g in rng.permutation(8)[:4]:
        for a in range(0, N, 4):
            z = rng.permutation(C)
            t = np.roll(z, -1)
            m[a:a + 2, g] = pairs(z[::2], z[1::2])
            m[a + 2:a + 4, g] = pairs(t[::2], t[1::2])
            x[a:a + 4, g, 0, 1, :, 0] = -1.0
            x[a:a + 2, g, 0, 1, t[::4], 0] = 1.0
            x[a + 2:a + 4, g, 0, 1, z[::4], 0] = 1.0
    u = d["u"].reshape(N, 128, 128, 4)
    u[:, :, ::16] = 0
    for h in range(0, 128, 16): u[:, h + 1, h, 0] = 1.0
    w = layers(rng)
    w[:, :, :, :, :, 1] = 0
    w[:, :, :, :, :, 8:] = 0
    return {"x": x.astype(np.float32).reshape(N, 128, 4 * C).astype(BF), "u": u.reshape(N, 128, 512), "v": d["v"], "m": np.stack([gtable(m[r]) for r in range(N)]), **weights(rng, w)}
def setup_inputs_ends(rng):
    d = numbers_of(rng)
    v = np.array(d["v"]).astype(np.float32)
    u = d["u"].reshape(N, 128, 128, 4)
    u[:, :, ::16] = 0
    x = np.zeros((N, 8, 16, C, 4), np.float32)
    w = np.zeros((N, 128, 4, 128, 4), np.float32)
    m = np.zeros((N, 8, C), np.int64)
    high = rng.random((N, 8, C)) < 0.5
    kind = rng.permutation(N // 2)
    n = np.arange(128)
    for i in range(N // 2):
        a, b = 2 * i, 2 * i + 1
        for g in range(8):
            if kind[i] == 1:
                m[a, g] = np.arange(C)[::-1] if g % 2 else np.arange(C) ^ 1
                m[b, g] = m[a, g]
                continue
            z = rng.permutation(C).reshape(-1, 4 if kind[i] == 3 else C)
            t = np.roll(z, -1, axis=1)
            m[a, g] = pairs(z[:, ::2], z[:, 1::2])
            m[b, g] = pairs(t[:, ::2], t[:, 1::2])
            high[a, g] = False
            high[b, g] = False
            high[a, g, t[:, ::4]] = True
            high[b, g, z[:, ::4]] = True
        one = a + int(rng.integers(2))
        whole = rng.permutation(8)
        for r in (a, b):
            large = kind[i] == 2 or (kind[i] < 2 and r == one)
            below = kind[i] == 1 and r == one
            top = -1.0 if below else -0.5 if r == one and kind[i] in (0, 2) else 1.0
            x[r] = ((2.0 ** 21 if large else 2.0 ** -27) * np.where(high[r], top, -0.75 if below else -1.0))[:, None, :, None]
            k = 2.0 ** 30 if large else 2.0 ** -30
            for h in range(0, 128, 16):
                u[r, h:h + 16, h] = k
                if below and whole[h // 16] < 4: u[r, :, h] = k
                elif below:
                    g = (h + 16) % 128
                    u[r, g:g + 16, h] = -k
            v[r] = k * (rng.integers(0, 2, v[r].shape) * 2.0 - 1.0)
            for c in range(4): w[r, n, c, n, c] = 128.0 if below else 128.0 * (rng.integers(0, 2) * 2.0 - 1.0)
    return {"x": x.reshape(N, 128, 4 * C).astype(BF), "u": u.reshape(N, 128, 512), "v": v.astype(BF), "m": np.stack([gtable(m[r]) for r in range(N)]), **weights(rng, w.astype(BF))}
def setup_inputs_spread(rng):
    d = setup_inputs(rng)
    d["x"] = big(wide(rng, N, 128, 4 * C, cols=6))
    return d
def check_inputs(d):
    b = []
    for k, low, top in (("x", 2.0 ** -27, 2.0 ** 21), ("u", 2.0 ** -30, 2.0 ** 30), ("v", 2.0 ** -30, 2.0 ** 30)):
        a = np.abs(d[k].astype(np.float32))
        if not (np.isfinite(a).all() and ((a == 0) | (a >= low) & (a <= top)).all()): b.append("a value of " + k)
    none, least, most = [emit(mx_ref.quantize(np.full((128, 16), k, np.float32).astype(BF)))[1][0, 0] for k in (0.0, 2.0 ** -30, 2.0 ** 30)]
    for r in range(N):
        e = gentries(d["m"][r])
        if ((e < 0) | (e >= C)).any(): b.append("an entry of m")
        elif (e == np.arange(C)).any() or (at(e, e) != np.arange(C)).any(): b.append("m: no pairing")
        if ((d["wc"][r] & 0x7F) == 0x7F).any(): b.append("wc: a code that is no number")
        s = mx_ref.live(d["ws"][r])
        if ((s != none) & ((s < least) | (s > most))).any(): b.append("ws: a scale out of range")
        a = np.abs(decode(pk(d["wc"][r], d["ws"][r])).astype(np.float64)).reshape(128, 512, 4)
        if not (np.sum(a, axis=(0, 2)) <= 128).all(): b.append("W: the sizes of a column")
    return b
def reference(x, u, v, m, wc, ws):
    qu = [mx_ref.quantize(u[r]) for r in range(N)]
    lay = [pk(wc[r], ws[r]) for r in range(N)]
    now = [x[r] for r in range(N)]
    mate = [gentries(m[r]) for r in range(N)]
    j = np.arange(C)
    for h in STRIDE:
        q = [mx_ref.quantize(now[r]) for r in range(N)]
        have = [decode(q[r]).astype(BF) for r in range(N)]
        made, mates = [], []
        for r in range(N):
            e = r ^ h
            o, p = mate[r], mate[e]
            s = mx_ref.matmul(qu[r], q[r])[::16] + np.float32(0.0)
            val, low = np.maximum(s, at(s, p)), np.minimum(j, p)
            beats = (val > at(val, o)) | ((val == at(val, o)) & (low < at(low, o)))
            app = beats & at(beats, p)
            n = np.where(app, p, np.where(at(app, o), at(o, at(p, o)), o))
            one, two, slot = np.full((8, K), -1), np.full((8, K), -1), np.full((8, C), -1)
            for g in range(8):
                a = np.flatnonzero(app[g] & (j < p[g]))
                one[g, :len(a)], two[g, :len(a)] = a, p[g][a]
                slot[g, a] = np.arange(len(a))
                slot[g, p[g][a]] = np.arange(len(a))
            came = decode(mx_ref.quantize(halved(gcols(have[e], one), gcols(have[e], two)))).astype(BF)
            add = gcols(came, slot).astype(np.float32)
            own = have[r].astype(np.float32)
            z = mx_ref.quantize(halved(gcols(have[r], o), gcols(have[r], n)))
            made.append(tile([(mx_ref.matmul(pick(lay[r], np.arange(128 * b, 128 * b + 128)), z) * np.float32(0.03125) + own[:, b::4]) + add[:, b::4] for b in range(4)]))
            mates.append(n)
        now, mate = made, mates
    y, om = np.zeros((N, 128, C), np.float32), np.zeros((N, 8, C), np.float32)
    oc, osc = np.zeros((N, 128, 4 * C), np.uint8), np.zeros((N, 16, C), np.uint8)
    for r in range(N):
        q = mx_ref.quantize(now[r])
        y[r] = mx_ref.matmul(mx_ref.quantize(v[r]), q)
        om[r] = mate[r]
        oc[r], osc[r] = emit(q)
    return {"y": y, "om": om, "oc": oc, "osc": osc}

@@ -1,0 +1,455 @@
+from concourse.bass import DstId, RemoteDMATransfer
+from concourse.mybir import dt, AluOpType, ActivationFunctionType
+
+C = 320
+KW = C // 16
+H = C // 2
+CZ = C + 16
+STRIDE = [1, 2, 4]
+Q4, U8, U16 = "float8_e4m3fn_x4", "uint8", "uint16"
+BF, F32, I32 = "bfloat16", "float32", "int32"
+
+SCRATCH = {
+    "x0": ("sbuf", [128, 4 * C], BF), "xt": ("sbuf", [128, 4 * C], BF),
+    "zt": ("sbuf", [128, 4 * C], BF), "at": ("sbuf", [128, 4 * C], BF),
+    "fh": ("sbuf", [128, 4 * C], BF), "fo": ("sbuf", [128, 4 * C], BF), "fp": ("sbuf", [128, 4 * CZ], BF),
+    "fa": ("sbuf", [128, 4 * C], BF),
+    "xq": ("sbuf", [128, 4 * C], Q4), "xs": ("sbuf", [128, 4 * C], U8),
+    "lq": ("sbuf", [128, 3 * C], Q4), "ls": ("sbuf", [128, 3 * C], U8),
+    "rq": ("sbuf", [128, H], Q4), "rs": ("sbuf", [128, H], U8),
+    "zq": ("sbuf", [128, C], Q4), "zs": ("sbuf", [128, C], U8),
+    "aq": ("sbuf", [128, C], Q4), "asc": ("sbuf", [128, C], U8),
+    "wq": ("sbuf", [128, 512], Q4), "wsc": ("sbuf", [128, 512], U8),
+    "ub": ("sbuf", [128, 512], BF), "uq": ("sbuf", [128, 128], Q4), "us": ("sbuf", [128, 128], U8),
+    "uq2": ("sbuf", [128, 128], Q4), "us2": ("sbuf", [128, 128], U8),
+    "vb": ("sbuf", [128, 512], BF), "vq": ("sbuf", [128, 128], Q4), "vs": ("sbuf", [128, 128], U8),
+    "eb": ("sbuf", [128, 2048], BF), "eq": ("sbuf", [128, 512], Q4), "es": ("sbuf", [128, 512], U8),
+    "di": ("sbuf", [128, 128], I32), "jrow": ("sbuf", [128, C], I32), "tm": ("sbuf", [128, C], I32),
+    "pmi": ("sbuf", [128, 1], I32), "cols": ("sbuf", [128, 8], F32),
+    "ra": ("sbuf", [128, C], BF), "rb": ("sbuf", [128, C], BF), "rr": ("sbuf", [128, C], BF),
+    "jf": ("sbuf", [128, C], F32), "jt": ("sbuf", [128, C], F32), "jw": ("sbuf", [128, KW], F32),
+    "uoff": ("sbuf", [128, 8], U16),
+    "md": ("dram", [128, KW], I32), "rmd": ("dram", [128, KW], I32),
+    "mi": ("sbuf", [128, KW], I32), "p0": ("sbuf", [128, KW], I32),
+    "ml": ("sbuf", [128, 8 * KW], U16), "pl0": ("sbuf", [128, 2 * KW], U16), "pl": ("sbuf", [128, 4 * KW], U16),
+    "al": ("sbuf", [128, KW], U16), "aj": ("sbuf", [128, KW], U16), "ajf": ("sbuf", [128, KW], F32),
+    "cj": ("sbuf", [128, KW], F32), "lowf": ("sbuf", [128, KW], F32),
+    "sc2": ("sbuf", [128, C], F32), "val2": ("sbuf", [128, C], F32), "bt2": ("sbuf", [128, C], BF),
+    "fw": ("sbuf", [128, C], BF), "lrow2": ("sbuf", [128, C], F32),
+    "d0": ("sbuf", [128, 7 * KW], F32), "d1": ("sbuf", [128, 7 * KW], F32), "f7": ("sbuf", [128, 7 * KW], F32),
+    "sc": ("sbuf", [128, C], F32), "val": ("sbuf", [128, C], F32), "dd": ("sbuf", [128, C], BF),
+    "tt": ("sbuf", [128, C], BF), "bt": ("sbuf", [128, C], BF), "app": ("sbuf", [128, C], BF),
+    "vv": ("sbuf", [128, C], BF), "fv": ("sbuf", [128, C], BF), "fk": ("sbuf", [128, C], F32),
+    "lrow": ("sbuf", [128, C], F32), "orow": ("sbuf", [128, C], F32), "oprow": ("sbuf", [128, C], F32),
+    "oporow": ("sbuf", [128, C], F32), "ysb": ("sbuf", [128, C], F32),
+    "ps_s": ("psum", [128, 512], F32), "ps_r": ("psum", [128, 2048], F32), "ps_p": ("psum", [128, 1536], F32),
+}
+SEMAPHORES = ["cv", "cs", "cp", "cg", "d_md", "d_mi", "d_x", "d_u", "d_v", "d_wc", "d_ws", "d_om", "d_oc", "d_y", "d_sc0",
+              "d_sc1", "d_sc2", "d_sc3", "sent0", "sent", "h_list", "h_code", "h_scale",
+              "a_list0", "a_list1", "a_list2", "a_code0", "a_code1", "a_code2", "a_scale0", "a_scale1", "a_scale2"]
+
+A = AluOpType
+COPY = ActivationFunctionType.Copy
+
+
+def bits(engines):
+    m = 0
+    for e in engines:
+        m |= 1 << e
+    return m
+
+
+def helpers(T, topo, src, dst):
+    able = [c for c in topo.cores_of(src) if T.rank_of(c) is None and topo.may_write(c, dst)]
+    near = [c for c in able if topo.die(c) == topo.die(src)]
+    far = [c for c in able if topo.die(c) != topo.die(src)]
+    return near[0], far[0]
+
+
+def hand_on(g, core, T, topo, src, dst, half):
+    rid, pid = topo.addr(dst, core)
+    mask, n = topo.mask(core, dst), len(topo.engines(core, dst))
+    nin = len(topo.engines(core, dst))
+    total = 0
+    if half == 0:
+        g.wait_ge(T.sem.h_list, nin)
+        g.remote_dma(T.p0[:], T.rmd[:], T.sem.a_list0, T.sem.sent, pid, rid, mask)
+        total += n
+    g.wait_ge(T.sem.h_code, nin // 2)
+    g.remote_dma(T.lq[:, half * H:half * H + H].bitcast(dt.uint8), T.rq[:].bitcast(dt.uint8), T.sem.a_code0, T.sem.sent, pid, rid, mask)
+    g.wait_ge(T.sem.h_scale, nin // 2)
+    g.remote_dma(T.ls[:, half * H:half * H + H], T.rs[:], T.sem.a_scale0, T.sem.sent, pid, rid, mask)
+    g.wait_ge(T.sem.sent, total + 2 * n)
+
+
+def rank_program(g, core, T, topo):
+    rank = T.rank_of(core)
+    if rank is None:
+        for r, c in enumerate(T.cores):
+            d = T.cores[r ^ STRIDE[0]]
+            if core in topo.cores_of(c) and not topo.may_write(c, d):
+                hs = helpers(T, topo, c, d)
+                if core in hs:
+                    hand_on(g, core, T, topo, c, d, hs.index(core))
+        return
+
+    eng = {"V": g.vector, "S": g.scalar, "P": g.tensor, "G": g, "Y": g.sync}
+    csem = {"V": "cv", "S": "cs", "P": "cp", "G": "cg"}
+    count, direct = {}, {}
+    known = {q: {} for q in eng}
+    wrote, readers = {}, {}
+
+    def need(q, reads, writes, chain=False):
+        deps = [wrote[k] for k in reads if k in wrote]
+        for k in writes:
+            if k in wrote and not chain:
+                deps.append(wrote[k])
+            deps += readers.get(k, [])
+        top = {}
+        for s, v, clk in deps:
+            if v > known[q].get(s, 0) and v > top.get(s, (0, None))[0]:
+                top[s] = (v, clk)
+        for s in sorted(top):
+            v, clk = top[s]
+            if any(o != s and top[o][1].get(s, 0) >= v for o in top):
+                continue
+            eng[q].wait_ge(T.sem[s], v)
+            direct[s] = max(direct.get(s, 0), v)
+        for s in top:
+            v, clk = top[s]
+            known[q][s] = max(known[q].get(s, 0), v)
+            for o in clk:
+                known[q][o] = max(known[q].get(o, 0), clk[o])
+
+    def done(q, s, n, reads, writes):
+        count[s] = count.get(s, 0) + n
+        ev = (s, count[s], dict(known[q]))
+        for k in reads:
+            readers.setdefault(k, []).append(ev)
+        for k in writes:
+            wrote[k] = ev
+            readers[k] = []
+
+    def op(q, call, reads, writes, chain=False):
+        need(q, reads, writes, chain)
+        call().then_inc(T.sem[csem[q]], 1)
+        done(q, csem[q], 1, reads, writes)
+
+    def dma(q, s, out, in_, reads, writes):
+        need(q, reads, writes)
+        eng[q].dma_start(out, in_).then_inc(T.sem[s], 16)
+        done(q, s, 16, reads, writes)
+
+    def lands(key, s, n):
+        count[s] = n
+        wrote[key] = (s, n, {})
+
+    V, S, P = g.vector, g.scalar, g.tensor
+
+    def ts(out, in0, s1, s2, op0, op1, reads, writes):
+        if op1 is None:
+            op("V", lambda: V.tensor_scalar(out, in0, s1, None, op0), reads, writes)
+        else:
+            op("V", lambda: V.tensor_scalar(out, in0, s1, s2, op0, op1), reads, writes)
+
+    def cp(out, in_, reads, writes):
+        op("V", lambda: V.tensor_copy(out, in_), reads, writes)
+
+    def tt(out, in0, in1, alu, reads, writes):
+        op("V", lambda: V.tensor_tensor(out, in0, in1, alu), reads, writes)
+
+    def act(out, in_, scale, reads, writes):
+        if scale is None:
+            op("S", lambda: S.activation(out, in_, COPY), reads, writes)
+        else:
+            op("S", lambda: S.activation(out, in_, COPY, scale=scale), reads, writes)
+
+    def quant(q, s, t, reads, writes):
+        op("V", lambda: V.quantize_mx(q, s, t), reads, writes)
+
+    def mm(out, lq, ls, rq, rs, start, stop, reads, bank):
+        op("P", lambda: P.matmul_mx(out, lq, ls, rq, rs, start, stop), reads, [bank], chain=not start)
+
+    def scan(out, d0, d1, reads, writes):
+        op("V", lambda: V.tensor_tensor_scan(out, d0, d1, 0.0, A.mult, A.add), reads, writes)
+
+    partner = [T.cores[rank ^ h] for h in STRIDE]
+    relay = None if topo.may_write(core, partner[0]) else helpers(T, topo, core, partner[0])
+    out_eng = topo.engines(relay[0] if relay else core, partner[0])
+    ne = len(out_eng)
+
+    def send(s_local, out, in_, s_remote, dst, reads):
+        need("G", reads, [])
+        rid, pid = topo.addr(dst, core)
+        g.remote_dma(out, in_, T.sem[s_remote], T.sem[s_local], pid, rid, bits(out_eng))
+        done("G", s_local, ne, [], [])
+
+    def send_halves(outs, ins, s_remote, reads):
+        need("G", reads, [])
+        tr = []
+        for i in range(2):
+            rid, pid = topo.addr(relay[i], core)
+            tr.append(RemoteDMATransfer(dst_ids=[DstId(rid=rid, pnc=pid)], dma_engine_mask=bits(out_eng[i::2]),
+                                        remote_sem=T.sem[s_remote], src=ins[i], dst=outs[i]))
+        g.remote_dma_fused(tr, local_sem=T.sem.sent0)
+        done("G", "sent0", ne, [], [])
+
+    for r in range(3):
+        k = 2 if (r == 0 and relay) else 1
+        lands("lq%d" % r, "a_code%d" % r, k * ne)
+        lands("ls%d" % r, "a_scale%d" % r, k * ne)
+    lands("p0", "a_list0", ne)
+    lands("P1", "a_list1", ne)
+    lands("P2", "a_list2", ne)
+
+    def xq(r):
+        return T.xq[:, r * C:(r + 1) * C], T.xs[:, r * C:(r + 1) * C]
+
+    def own(r):
+        return T.ml[:, 2 * KW * r:2 * KW * r + KW]
+
+    def plist(r, low=0):
+        if r == 0:
+            return T.pl0[:, low * KW:low * KW + KW]
+        return T.pl[:, 2 * KW * (r - 1) + low * KW:2 * KW * (r - 1) + low * KW + KW]
+
+    def plane(t, b, w=C):
+        return t[:, b * w:b * w + C]
+
+    def bank(t, b):
+        return t[:, 512 * b:512 * b + C]
+
+    def ecol(b):
+        return T.eq[:, 128 * b:128 * b + 128], T.es[:, 128 * b:128 * b + 128]
+
+    pmf, pm1, thr, inv = [T.cols[:, i:i + 1] for i in range(4)]
+    W7 = 7 * KW
+
+    dma("Y", "d_md", T.md[:], T.m[:], [], ["md"])
+    dma("S", "d_x", T.x0[:], T.x[:], [], ["x0"])
+    dma("Y", "d_mi", T.mi[:], T.m[:], [], ["mi"])
+    dma("Y", "d_u", T.ub[:], T.u[:], [], ["ub"])
+    op("G", lambda: g.iota(T.di[:], [[-1, 128]], 0, 1), [], ["di"])
+    op("G", lambda: g.iota(T.jrow[:], [[1, C]], 0, 0), [], ["jrow"])
+    if relay:
+        send("sent0", T.rmd[:], T.md[:], "h_list", relay[0], ["md"])
+    else:
+        send("sent0", T.p0[:], T.md[:], "a_list0", partner[0], ["md"])
+    need("Y", ["x0"], [])
+    dma("Y", "d_v", T.vb[:], T.v[:], [], ["vb"])
+
+    op("V", lambda: V.memset(T.eb[:], 0.0), [], ["eb%d" % b for b in range(4)])
+    op("V", lambda: V.memset(T.d0[:], -1.0), [], ["d0c", "d0a", "d0b", "d0d"])
+    ts(T.pmi[:], T.di[:, 0:1], 15, None, A.bitwise_and, None, ["di"], ["pmi"])
+    for b in range(4):
+        ts(T.eb[:, 512 * b + b:512 * b + 512:4], T.di[:], 0.0, 32.0, A.is_equal, A.mult, ["di"], ["eb%d" % b])
+    ts(T.d0[:, 0:W7:7], T.di[:, 0:KW], 0.0, None, A.mult, None, ["di"], ["d0c"])
+    cp(pmf, T.pmi[:], ["pmi"], ["pmf"])
+    cp(T.uoff[:], T.jrow[:, 0:128:16], ["jrow"], ["uoff"])
+    cp(own(0), T.mi[:], ["mi"], ["M0"])
+    cp(T.jf[:], T.jrow[:], ["jrow"], ["jf"])
+    quant(T.eq[:], T.es[:], T.eb[:], ["eb%d" % b for b in range(4)], ["eq"])
+
+    def head(r):
+        q, s = xq(r)
+        if r == 0:
+            quant(q, s, T.x0[:], ["x0"], ["xq0"])
+        else:
+            quant(q, s, T.xt[:], ["xt%d" % b for b in range(4)], ["xq%d" % r])
+        if r == 3:
+            return
+        if r == 0 and relay:
+            send_halves([T.rq[:].bitcast(dt.uint8)] * 2, [T.xq[:, i * H:i * H + H].bitcast(dt.uint8) for i in range(2)], "h_code", ["xq0"])
+            send_halves([T.rs[:]] * 2, [T.xs[:, i * H:i * H + H] for i in range(2)], "h_scale", ["xq0"])
+        else:
+            sl = "sent0" if r == 0 else "sent"
+            send(sl, T.lq[:, r * C:(r + 1) * C].bitcast(dt.uint8), q.bitcast(dt.uint8), "a_code%d" % r, partner[r], ["xq%d" % r])
+            send(sl, T.ls[:, r * C:(r + 1) * C], s, "a_scale%d" % r, partner[r], ["xq%d" % r])
+
+    head(0)
+    wrote["sent0"] = ("sent0", count["sent0"], {})
+    dma("Y", "d_wc", T.wq[:].bitcast(dt.uint8), T.wc[:], ["sent0"], ["wq"])
+    dma("Y", "d_ws", T.wsc[:], T.ws[:], [], ["wsc"])
+
+    quant(T.uq[:], T.us[:], T.ub[:], ["ub"], ["uq"])
+    ts(pm1, T.pmi[:], 1.0, None, A.add, None, ["pmi"], ["pm1"])
+    cp(T.uq2[:].bitcast(dt.uint32), T.uq[:].bitcast(dt.uint32).indirect(T.uoff[:]), ["uq", "uoff"], ["uq2"])
+    cp(T.us2[:], T.us[:].indirect(T.uoff[:]), ["uq", "uoff"], ["us2"])
+    ts(T.tm[:], T.jrow[:], 15, None, A.bitwise_and, None, ["jrow"], ["tm"])
+    ts(T.jw[:], T.jrow[:, 0:C:16], pmf, None, A.add, None, ["jrow", "pmf"], ["jw"])
+    ts(T.d1[:, 5:W7:7], T.jrow[:, 0:KW], 0.0, float(C), A.mult, A.add, ["jrow"], ["d1c"])
+    ts(T.d1[:, 6:W7:7], T.jrow[:, 0:KW], 0.0, float(C), A.mult, A.add, ["jrow"], ["d1e"])
+    for b in range(4):
+        op("V", lambda: V.memset(T.fp[:, CZ * b + C:CZ * b + CZ], 0.0), [], ["fz%d" % b])
+    ts(T.cj[:], T.jw[:], -1.0, float(C), A.mult, A.add, ["jw"], ["cj"])
+    ts(T.ra[:], T.tm[:], pm1, 2.0 ** 60, A.is_equal, A.mult, ["tm", "pm1"], ["ra"])
+    ts(T.rb[:], T.tm[:], pmf, None, A.not_equal, None, ["tm", "pmf"], ["rb"])
+    ts(thr, T.pmi[:], -15.005, -100.0, A.add, A.mult, ["pmi"], ["thr"])
+    ts(inv, T.pmi[:], 15.0, 2.0 ** -60, A.is_equal, A.add, ["pmi"], ["inv"])
+    cp(T.d1[:, 1:W7:7], T.mi[:], ["mi"], ["d1o1"])
+    cp(T.d1[:, 2:W7:7], T.mi[:], ["mi"], ["d1o2"])
+    tt(T.rr[:], T.ra[:], T.rb[:], A.add, ["ra", "rb"], ["rr"])
+    quant(T.vq[:], T.vs[:], T.vb[:], ["vb"], ["vq"])
+    act(T.jt[:], T.jf[:], 2.0 ** -120, ["jf"], ["jt"])
+
+    def o_row(r):
+        act(T.orow[:], T.jf[:].indirect(own(r)), None, ["jf", "M%d" % r], ["orow"])
+
+    def low_row(r):
+        act(T.lrow[:], T.jt[:].indirect(plist(r, 1)), None, ["jt", "L0" if r == 0 else "P%d" % r], ["lrow"])
+
+    def low_copy():
+        act(T.lrow2[:], T.lrow[:], None, ["lrow"], ["lrow2"])
+
+    def op_row(r):
+        act(T.oprow[:], T.orow[:].indirect(plist(r)), None, ["orow", "P%d" % r], ["oprow"])
+
+    def opo_row(r):
+        act(T.oporow[:], T.oprow[:].indirect(own(r)), None, ["oprow", "M%d" % r], ["oporow"])
+
+    o_row(0)
+
+    for r in range(3):
+        q, s = xq(r)
+        XQ, M, PK = "xq%d" % r, "M%d" % r, "P%d" % r
+        o, p = own(r), plist(r)
+        mm(T.ps_s[:, 0:C], T.uq2[:], T.us2[:], q, s, True, True, ["uq2", "us2", XQ], "ps_s")
+        for b in range(4):
+            mm(bank(T.ps_r, b), *ecol(b), q, s, True, True, ["eq", XQ], "ps_r%d" % b)
+        if r > 0:
+            opo_row(r)
+        act(T.sc[:], T.ps_s[:, 0:C], None, [], ["ps_s", "sc"])
+        act(T.sc2[:], T.ps_s[:, 0:C], None, [], ["ps_s", "sc2"])
+        for b in range(4):
+            act(plane(T.fh, b), bank(T.ps_r, b), 2.0 ** -6, [], ["ps_r%d" % b, "fh%d" % b])
+        for b in range(4):
+            act(plane(T.fo, b), plane(T.fh, b).indirect(o), None, ["fh%d" % b, M], ["fo%d" % b])
+
+        def t_op():
+            tt(T.tt[:], T.lrow[:].indirect(o), T.lrow2[:], A.subtract, ["lrow", "lrow2", M], ["tt"])
+
+        def val_op():
+            tt(T.val[:], T.sc[:].indirect(p), T.sc2[:], A.max, ["sc", "sc2", PK], ["val"])
+
+        def val_copy():
+            cp(T.val2[:], T.val[:], ["val"], ["val2"])
+
+        def d_op():
+            tt(T.dd[:], T.val[:].indirect(o), T.val2[:], A.subtract, ["val", "val2", M], ["dd"])
+
+        def beats_op():
+            tt(T.bt[:], T.dd[:], T.tt[:], A.is_lt, ["dd", "tt"], ["bt"])
+
+        def beats_copy():
+            cp(T.bt2[:], T.bt[:], ["bt"], ["bt2"])
+
+        def app_op():
+            tt(T.app[:], T.bt[:].indirect(p), T.bt2[:], A.mult, ["bt", "bt2", PK], ["app"])
+
+        def v_op():
+            cp(T.vv[:], T.app[:].indirect(o), ["app", M], ["vv"])
+
+        def scan_a():
+            scan(T.fw[:], T.rr[:], T.app[:], ["rr", "app"], ["fw"])
+
+        def scan_k():
+            scan(T.fk[:], T.rr[:], T.oporow[:], ["rr", "oporow"], ["fk"])
+
+        def opo_op():
+            ts(T.d1[:, 0:W7:7], T.fk[:, 15:C:16], inv, None, A.mult, None, ["fk", "inv"], ["d1k"])
+
+        def p_op(i):
+            cp(T.d1[:, 3 + i:W7:7], p, [PK], ["d1p%d" % i])
+
+        def o_op(i):
+            cp(T.d1[:, i:W7:7], T.f7[:, 4:W7:7], ["f7"], ["d1o%d" % i])
+
+        def scan_v():
+            scan(T.fv[:], T.rr[:], T.vv[:], ["rr", "vv"], ["fv"])
+
+        if r == 0:
+            cp(p, T.p0[:], ["p0"], ["P0"])
+            tt(T.lowf[:], T.p0[:], T.jw[:], A.min, ["p0", "jw"], ["lowf"])
+            cp(plist(0, 1), T.lowf[:], ["lowf"], ["L0"])
+            low_row(0)
+            low_copy()
+            op_row(0)
+            opo_row(0)
+            val_op(), p_op(0), val_copy(), p_op(1), d_op(), t_op(), beats_op(), beats_copy(), app_op()
+            scan_k(), v_op(), scan_a(), scan_v(), opo_op()
+        else:
+            t_op(), scan_k(), val_op(), opo_op(), val_copy(), p_op(0), d_op(), p_op(1), beats_op(), o_op(1), beats_copy(), o_op(2)
+            app_op(), v_op(), scan_a(), scan_v()
+        fv, fw = T.fv[:, 15:C:16], T.fw[:, 15:C:16]
+        ts(T.d0[:, 4:W7:7], fw, thr, -1.0, A.is_ge, A.add, ["fw", "thr"], ["d0b"])
+        ts(T.d0[:, 6:W7:7], fw, thr, -1.0, A.is_ge, A.mult, ["fw", "thr"], ["d0d"])
+        ts(T.d0[:, 2:W7:7], fv, thr, -1.0, A.is_ge, A.mult, ["fv", "thr"], ["d0a"])
+        scan(T.f7[:], T.d0[:], T.d1[:], ["d0c", "d0a", "d0b", "d0d", "d1k", "d1o1", "d1o2", "d1p0", "d1p1", "d1c", "d1e"], ["f7"])
+        MN, n = "M%d" % (r + 1), own(r + 1)
+        cp(n, T.f7[:, 4:W7:7], ["f7"], [MN])
+
+        def z_op(b):
+            tt(T.zt[:, b:4 * C:4], plane(T.fh, b).indirect(n), plane(T.fo, b), A.add, ["fh%d" % b, "fo%d" % b, MN], ["zt%d" % b])
+
+        tt(T.ajf[:], T.d0[:, 6:W7:7], T.cj[:], A.mult, ["d0d", "cj"], ["ajf"])
+        if r < 2:
+            tt(T.lowf[:], T.f7[:, 4:W7:7], T.jw[:], A.min, ["f7", "jw"], ["lowf"])
+        z_op(0)
+        ts(T.aj[:], T.ajf[:], float(C), None, A.add, None, ["ajf"], ["aj"])
+        if r < 2:
+            a = 2 * KW * (r + 1)
+            cp(T.ml[:, a + KW:a + 2 * KW], T.lowf[:], ["lowf"], ["ML%d" % r])
+            send("sent", T.pl[:, 2 * KW * r:2 * KW * (r + 1)], T.ml[:, a:a + 2 * KW], "a_list%d" % (r + 1), partner[r + 1], [MN, "ML%d" % r])
+        z_op(1), z_op(2), z_op(3)
+        cp(T.al[:], T.f7[:, 6:W7:7], ["f7"], ["al"])
+        quant(T.zq[:], T.zs[:], T.zt[:], ["zt%d" % b for b in range(4)], ["zq"])
+
+        lq, ls = T.lq[:, r * C:(r + 1) * C], T.ls[:, r * C:(r + 1) * C]
+
+        def f_mm(b):
+            mm(bank(T.ps_p, b % 3), *ecol(b), lq, ls, True, True, ["eq", "lq%d" % r, "ls%d" % r], "ps_p%d" % (b % 3))
+
+        def f_copy(b):
+            act(plane(T.fp, b, CZ), bank(T.ps_p, b % 3), 2.0 ** -6, [], ["ps_p%d" % (b % 3), "fp%d" % b])
+
+        f_mm(0), f_mm(1), f_mm(2), f_copy(0), f_mm(3), f_copy(1), f_copy(2), f_copy(3)
+        for b in range(4):
+            act(plane(T.fa, b), T.fp[:, CZ * b:CZ * b + CZ].indirect(T.aj[:]), None, ["fp%d" % b, "fz%d" % b, "aj"], ["fa%d" % b])
+
+        for b in range(4):
+            mm(bank(T.ps_r, b), *ecol(b), q, s, True, False, ["eq", XQ], "ps_r%d" % b)
+        for b in range(4):
+            mm(bank(T.ps_r, b), T.wq[:, 128 * b:128 * b + 128], T.wsc[:, 128 * b:128 * b + 128], T.zq[:], T.zs[:], False, False,
+               ["wq", "wsc", "zq"], "ps_r%d" % b)
+        for b in range(4):
+            tt(T.at[:, b:4 * C:4], T.fp[:, CZ * b:CZ * b + CZ].indirect(T.al[:]), plane(T.fa, b), A.add,
+               ["fp%d" % b, "fz%d" % b, "fa%d" % b, "al"], ["at%d" % b])
+        quant(T.aq[:], T.asc[:], T.at[:], ["at%d" % b for b in range(4)], ["aq"])
+        for b in range(4):
+            mm(bank(T.ps_r, b), *ecol(b), T.aq[:], T.asc[:], False, True, ["eq", "aq"], "ps_r%d" % b)
+
+        o_row(r + 1)
+        if r < 2:
+            low_row(r + 1)
+            op_row(r + 1)
+            low_copy()
+        else:
+            dma("Y", "d_om", T.om[:], T.orow[0:128:16, :], ["orow"], [])
+        for b in range(4):
+            if b % 2 == 0:
+                ts(T.xt[:, b:4 * C:4], bank(T.ps_r, b), 2.0 ** -5, None, A.mult, None, [], ["ps_r%d" % b, "xt%d" % b])
+            else:
+                act(T.xt[:, b:4 * C:4], bank(T.ps_r, b), 2.0 ** -5, [], ["ps_r%d" % b, "xt%d" % b])
+        head(r + 1)
+
+    q, s = xq(3)
+    mm(T.ps_s[:, 0:C], T.vq[:], T.vs[:], q, s, True, True, ["vq", "xq3"], "ps_s")
+    dma("Y", "d_oc", T.oc[:], q.bitcast(dt.uint8), ["xq3"], [])
+    cp(T.ysb[:], T.ps_s[:, 0:C], [], ["ps_s", "ysb"])
+    for k in range(4):
+        dma("S", "d_sc%d" % k, T.osc[4 * k:4 * k + 4, :], T.xs[32 * k:32 * k + 4, 3 * C:4 * C], ["xq3"], [])
+    dma("Y", "d_y", T.y[:], T.ysb[:], ["ysb"], [])
+    last = ["d_oc", "d_sc0", "d_sc1", "d_sc2", "d_sc3", "d_y"]
+    for s in sorted(count, key=lambda s: (last.index(s) if s in last else -1, s)):
+        if direct.get(s, 0) < count[s]:
+            g.wait_ge(T.sem[s], count[s])

@@ -6,6 +6,7 @@ KW = C // 16
 H = C // 2
 CZ = C + 16
 STRIDE = [1, 2, 4]
+LIST_ENG = 2
 Q4, U8, U16 = "float8_e4m3fn_x4", "uint8", "uint16"
 BF, F32, I32 = "bfloat16", "float32", "int32"
 
@@ -44,7 +45,7 @@ SCRATCH = {
     "oporow": ("sbuf", [128, C], F32), "ysb": ("sbuf", [128, C], F32),
     "ps_s": ("psum", [128, 512], F32), "ps_r": ("psum", [128, 2048], F32), "ps_p": ("psum", [128, 1536], F32),
 }
-SEMAPHORES = ["cv", "cs", "cp", "cg", "d_md", "d_mi", "d_x", "d_u", "d_v", "d_wc", "d_ws", "d_om", "d_oc", "d_y", "d_sc0",
+SEMAPHORES = ["cv", "cs", "cp", "cg", "d_md", "d_mi", "d_x", "d_u", "d_v", "d_wc", "d_ws", "d_om", "d_oc", "d_y", "d_y2", "d_sc0",
               "d_sc1", "d_sc2", "d_sc3", "sent0", "sent", "h_list", "h_code", "h_scale",
               "a_list0", "a_list1", "a_list2", "a_code0", "a_code1", "a_code2", "a_scale0", "a_scale1", "a_scale2"]
 
@@ -72,7 +73,7 @@ def hand_on(g, core, T, topo, src, dst, half):
     nin = len(topo.engines(core, dst))
     total = 0
     if half == 0:
-        g.wait_ge(T.sem.h_list, nin)
+        g.wait_ge(T.sem.h_list, LIST_ENG)
         g.remote_dma(T.p0[:], T.rmd[:], T.sem.a_list0, T.sem.sent, pid, rid, mask)
         total += n
     g.wait_ge(T.sem.h_code, nin // 2)
@@ -178,11 +179,11 @@ def rank_program(g, core, T, topo):
     out_eng = topo.engines(relay[0] if relay else core, partner[0])
     ne = len(out_eng)
 
-    def send(s_local, out, in_, s_remote, dst, reads):
+    def send(s_local, out, in_, s_remote, dst, reads, engines=out_eng):
         need("G", reads, [])
         rid, pid = topo.addr(dst, core)
-        g.remote_dma(out, in_, T.sem[s_remote], T.sem[s_local], pid, rid, bits(out_eng))
-        done("G", s_local, ne, [], [])
+        g.remote_dma(out, in_, T.sem[s_remote], T.sem[s_local], pid, rid, bits(engines))
+        done("G", s_local, len(engines), [], [])
 
     def send_halves(outs, ins, s_remote, reads):
         need("G", reads, [])
@@ -232,11 +233,9 @@ def rank_program(g, core, T, topo):
     op("G", lambda: g.iota(T.di[:], [[-1, 128]], 0, 1), [], ["di"])
     op("G", lambda: g.iota(T.jrow[:], [[1, C]], 0, 0), [], ["jrow"])
     if relay:
-        send("sent0", T.rmd[:], T.md[:], "h_list", relay[0], ["md"])
+        send("sent0", T.rmd[:], T.md[:], "h_list", relay[0], ["md"], out_eng[:LIST_ENG])
     else:
         send("sent0", T.p0[:], T.md[:], "a_list0", partner[0], ["md"])
-    need("Y", ["x0"], [])
-    dma("Y", "d_v", T.vb[:], T.v[:], [], ["vb"])
 
     op("V", lambda: V.memset(T.eb[:], 0.0), [], ["eb%d" % b for b in range(4)])
     op("V", lambda: V.memset(T.d0[:], -1.0), [], ["d0c", "d0a", "d0b", "d0d"])
@@ -266,15 +265,16 @@ def rank_program(g, core, T, topo):
             send(sl, T.lq[:, r * C:(r + 1) * C].bitcast(dt.uint8), q.bitcast(dt.uint8), "a_code%d" % r, partner[r], ["xq%d" % r])
             send(sl, T.ls[:, r * C:(r + 1) * C], s, "a_scale%d" % r, partner[r], ["xq%d" % r])
 
-    head(0)
-    wrote["sent0"] = ("sent0", count["sent0"], {})
-    dma("Y", "d_wc", T.wq[:].bitcast(dt.uint8), T.wc[:], ["sent0"], ["wq"])
-    dma("Y", "d_ws", T.wsc[:], T.ws[:], [], ["wsc"])
-
     quant(T.uq[:], T.us[:], T.ub[:], ["ub"], ["uq"])
     ts(pm1, T.pmi[:], 1.0, None, A.add, None, ["pmi"], ["pm1"])
     cp(T.uq2[:].bitcast(dt.uint32), T.uq[:].bitcast(dt.uint32).indirect(T.uoff[:]), ["uq", "uoff"], ["uq2"])
     cp(T.us2[:], T.us[:].indirect(T.uoff[:]), ["uq", "uoff"], ["us2"])
+    head(0)
+    wrote["sent0"] = ("sent0", count["sent0"], {})
+    dma("Y", "d_wc", T.wq[:].bitcast(dt.uint8), T.wc[:], ["sent0"], ["wq"])
+    dma("Y", "d_ws", T.wsc[:], T.ws[:], [], ["wsc"])
+    dma("Y", "d_v", T.vb[:], T.v[:], [], ["vb"])
+
     ts(T.tm[:], T.jrow[:], 15, None, A.bitwise_and, None, ["jrow"], ["tm"])
     ts(T.jw[:], T.jrow[:, 0:C:16], pmf, None, A.add, None, ["jrow", "pmf"], ["jw"])
     ts(T.d1[:, 5:W7:7], T.jrow[:, 0:KW], 0.0, float(C), A.mult, A.add, ["jrow"], ["d1c"])
@@ -289,7 +289,6 @@ def rank_program(g, core, T, topo):
     cp(T.d1[:, 1:W7:7], T.mi[:], ["mi"], ["d1o1"])
     cp(T.d1[:, 2:W7:7], T.mi[:], ["mi"], ["d1o2"])
     tt(T.rr[:], T.ra[:], T.rb[:], A.add, ["ra", "rb"], ["rr"])
-    quant(T.vq[:], T.vs[:], T.vb[:], ["vb"], ["vq"])
     act(T.jt[:], T.jf[:], 2.0 ** -120, ["jf"], ["jt"])
 
     def o_row(r):
@@ -314,19 +313,24 @@ def rank_program(g, core, T, topo):
         XQ, M, PK = "xq%d" % r, "M%d" % r, "P%d" % r
         o, p = own(r), plist(r)
         mm(T.ps_s[:, 0:C], T.uq2[:], T.us2[:], q, s, True, True, ["uq2", "us2", XQ], "ps_s")
+        mm(bank(T.ps_p, 2), T.uq2[:], T.us2[:], q, s, True, True, ["uq2", "us2", XQ], "ps_p2")
         for b in range(4):
             mm(bank(T.ps_r, b), *ecol(b), q, s, True, True, ["eq", XQ], "ps_r%d" % b)
-        if r > 0:
-            opo_row(r)
-        act(T.sc[:], T.ps_s[:, 0:C], None, [], ["ps_s", "sc"])
-        act(T.sc2[:], T.ps_s[:, 0:C], None, [], ["ps_s", "sc2"])
-        for b in range(4):
+
+        def s_op():
+            act(T.sc[:], T.ps_s[:, 0:C], None, [], ["ps_s", "sc"])
+
+        def s_copy():
+            cp(T.sc2[:], bank(T.ps_p, 2), [], ["ps_p2", "sc2"])
+
+        def fh_op(b):
             act(plane(T.fh, b), bank(T.ps_r, b), 2.0 ** -6, [], ["ps_r%d" % b, "fh%d" % b])
-        for b in range(4):
+
+        def fo_op(b):
             act(plane(T.fo, b), plane(T.fh, b).indirect(o), None, ["fh%d" % b, M], ["fo%d" % b])
 
-        def t_op():
-            tt(T.tt[:], T.lrow[:].indirect(o), T.lrow2[:], A.subtract, ["lrow", "lrow2", M], ["tt"])
+        def t_op(k):
+            tt(T.tt[:], T.lrow[:].indirect(own(k)), T.lrow2[:], A.subtract, ["lrow", "lrow2", "M%d" % k], ["tt"])
 
         def val_op():
             tt(T.val[:], T.sc[:].indirect(p), T.sc2[:], A.max, ["sc", "sc2", PK], ["val"])
@@ -347,7 +351,10 @@ def rank_program(g, core, T, topo):
             tt(T.app[:], T.bt[:].indirect(p), T.bt2[:], A.mult, ["bt", "bt2", PK], ["app"])
 
         def v_op():
-            cp(T.vv[:], T.app[:].indirect(o), ["app", M], ["vv"])
+            if r:
+                act(T.vv[:], T.app[:].indirect(o), None, ["app", M], ["vv"])
+            else:
+                cp(T.vv[:], T.app[:].indirect(o), ["app", M], ["vv"])
 
         def scan_a():
             scan(T.fw[:], T.rr[:], T.app[:], ["rr", "app"], ["fw"])
@@ -368,6 +375,7 @@ def rank_program(g, core, T, topo):
             scan(T.fv[:], T.rr[:], T.vv[:], ["rr", "vv"], ["fv"])
 
         if r == 0:
+            s_op(), s_copy(), fh_op(0), fh_op(1), fh_op(2), fh_op(3), fo_op(0), fo_op(1)
             cp(p, T.p0[:], ["p0"], ["P0"])
             tt(T.lowf[:], T.p0[:], T.jw[:], A.min, ["p0", "jw"], ["lowf"])
             cp(plist(0, 1), T.lowf[:], ["lowf"], ["L0"])
@@ -375,11 +383,13 @@ def rank_program(g, core, T, topo):
             low_copy()
             op_row(0)
             opo_row(0)
-            val_op(), p_op(0), val_copy(), p_op(1), d_op(), t_op(), beats_op(), beats_copy(), app_op()
+            fo_op(2), fo_op(3)
+            val_op(), p_op(0), val_copy(), p_op(1), d_op(), t_op(0), beats_op(), beats_copy(), app_op()
             scan_k(), v_op(), scan_a(), scan_v(), opo_op()
         else:
-            t_op(), scan_k(), val_op(), opo_op(), val_copy(), p_op(0), d_op(), p_op(1), beats_op(), o_op(1), beats_copy(), o_op(2)
-            app_op(), v_op(), scan_a(), scan_v()
+            op_row(r), s_op(), fh_op(0), fh_op(1), fh_op(2), fh_op(3), fo_op(0), opo_row(r), fo_op(1)
+            p_op(0), p_op(1), s_copy(), val_op(), o_op(1), val_copy(), o_op(2), d_op(), beats_op(), beats_copy(), app_op()
+            v_op(), fo_op(2), fo_op(3), scan_a(), scan_k(), opo_op(), scan_v()
         fv, fw = T.fv[:, 15:C:16], T.fw[:, 15:C:16]
         ts(T.d0[:, 4:W7:7], fw, thr, -1.0, A.is_ge, A.add, ["fw", "thr"], ["d0b"])
         ts(T.d0[:, 6:W7:7], fw, thr, -1.0, A.is_ge, A.mult, ["fw", "thr"], ["d0d"])
@@ -428,12 +438,11 @@ def rank_program(g, core, T, topo):
         for b in range(4):
             mm(bank(T.ps_r, b), *ecol(b), T.aq[:], T.asc[:], False, True, ["eq", "aq"], "ps_r%d" % b)
 
-        o_row(r + 1)
         if r < 2:
-            low_row(r + 1)
-            op_row(r + 1)
-            low_copy()
+            low_row(r + 1), low_copy(), t_op(r + 1), o_row(r + 1)
         else:
+            quant(T.vq[:], T.vs[:], T.vb[:], ["vb"], ["vq"])
+            o_row(r + 1)
             dma("Y", "d_om", T.om[:], T.orow[0:128:16, :], ["orow"], [])
         for b in range(4):
             if b % 2 == 0:
@@ -443,13 +452,16 @@ def rank_program(g, core, T, topo):
         head(r + 1)
 
     q, s = xq(3)
-    mm(T.ps_s[:, 0:C], T.vq[:], T.vs[:], q, s, True, True, ["vq", "xq3"], "ps_s")
+    mm(T.ps_s[:, 0:H], T.vq[:], T.vs[:], T.xq[:, 3 * C:3 * C + H], T.xs[:, 3 * C:3 * C + H], True, True, ["vq", "xq3"], "ps_s")
+    mm(T.ps_p[:, 0:H], T.vq[:], T.vs[:], T.xq[:, 3 * C + H:4 * C], T.xs[:, 3 * C + H:4 * C], True, True, ["vq", "xq3"], "ps_p0")
     dma("Y", "d_oc", T.oc[:], q.bitcast(dt.uint8), ["xq3"], [])
-    cp(T.ysb[:], T.ps_s[:, 0:C], [], ["ps_s", "ysb"])
     for k in range(4):
-        dma("S", "d_sc%d" % k, T.osc[4 * k:4 * k + 4, :], T.xs[32 * k:32 * k + 4, 3 * C:4 * C], ["xq3"], [])
-    dma("Y", "d_y", T.y[:], T.ysb[:], ["ysb"], [])
-    last = ["d_oc", "d_sc0", "d_sc1", "d_sc2", "d_sc3", "d_y"]
+        dma("YS"[k // 2], "d_sc%d" % k, T.osc[4 * k:4 * k + 4, :], T.xs[32 * k:32 * k + 4, 3 * C:4 * C], ["xq3"], [])
+    cp(T.ysb[:, H:C], T.ps_p[:, 0:H], [], ["ps_p0", "ysb1"])
+    act(T.ysb[:, 0:H], T.ps_s[:, 0:H], None, [], ["ps_s", "ysb0"])
+    dma("S", "d_y", T.y[:, 0:H], T.ysb[:, 0:H], ["ysb0"], [])
+    dma("Y", "d_y2", T.y[:, H:C], T.ysb[:, H:C], ["ysb1"], [])
+    last = ["d_oc", "d_sc0", "d_sc1", "d_sc2", "d_sc3", "d_y", "d_y2"]
     for s in sorted(count, key=lambda s: (last.index(s) if s in last else -1, s)):
         if direct.get(s, 0) < count[s]:
             g.wait_ge(T.sem[s], count[s])

from concourse.bass import DstId, RemoteDMATransfer
from concourse.mybir import dt, AluOpType, ActivationFunctionType

C = 320
KW = C // 16
H = C // 2
CZ = C + 16
STRIDE = [1, 2, 4]
LIST_ENG = 2
Q4, U8, U16 = "float8_e4m3fn_x4", "uint8", "uint16"
BF, F32, I32 = "bfloat16", "float32", "int32"

SCRATCH = {
    "x0": ("sbuf", [128, 4 * C], BF), "xt": ("sbuf", [128, 4 * C], BF),
    "zt": ("sbuf", [128, 4 * C], BF), "at": ("sbuf", [128, 4 * C], BF),
    "fh": ("sbuf", [128, 4 * C], BF), "fo": ("sbuf", [128, 4 * C], BF), "fp": ("sbuf", [128, 4 * CZ], BF),
    "fa": ("sbuf", [128, 4 * C], BF),
    "xq": ("sbuf", [128, 4 * C], Q4), "xs": ("sbuf", [128, 4 * C], U8),
    "lq": ("sbuf", [128, 3 * C], Q4), "ls": ("sbuf", [128, 3 * C], U8),
    "rq": ("sbuf", [128, H], Q4), "rs": ("sbuf", [128, H], U8),
    "zq": ("sbuf", [128, C], Q4), "zs": ("sbuf", [128, C], U8),
    "aq": ("sbuf", [128, C], Q4), "asc": ("sbuf", [128, C], U8),
    "wq": ("sbuf", [128, 512], Q4), "wsc": ("sbuf", [128, 512], U8),
    "ub": ("sbuf", [128, 512], BF), "uq": ("sbuf", [128, 128], Q4), "us": ("sbuf", [128, 128], U8),
    "uq2": ("sbuf", [128, 128], Q4), "us2": ("sbuf", [128, 128], U8),
    "vb": ("sbuf", [128, 512], BF), "vq": ("sbuf", [128, 128], Q4), "vs": ("sbuf", [128, 128], U8),
    "eb": ("sbuf", [128, 2048], BF), "eq": ("sbuf", [128, 512], Q4), "es": ("sbuf", [128, 512], U8),
    "di": ("sbuf", [128, 128], I32), "jrow": ("sbuf", [128, C], I32), "tm": ("sbuf", [128, C], I32),
    "pmi": ("sbuf", [128, 1], I32), "cols": ("sbuf", [128, 8], F32),
    "ra": ("sbuf", [128, C], BF), "rb": ("sbuf", [128, C], BF), "rr": ("sbuf", [128, C], BF),
    "jf": ("sbuf", [128, C], F32), "jt": ("sbuf", [128, C], F32), "jw": ("sbuf", [128, KW], F32),
    "uoff": ("sbuf", [128, 8], U16),
    "md": ("dram", [128, KW], I32), "rmd": ("dram", [128, KW], I32),
    "mi": ("sbuf", [128, KW], I32), "p0": ("sbuf", [128, KW], I32),
    "ml": ("sbuf", [128, 8 * KW], U16), "pl0": ("sbuf", [128, 2 * KW], U16), "pl": ("sbuf", [128, 4 * KW], U16),
    "al": ("sbuf", [128, KW], U16), "aj": ("sbuf", [128, KW], U16), "ajf": ("sbuf", [128, KW], F32),
    "cj": ("sbuf", [128, KW], F32), "lowf": ("sbuf", [128, KW], F32),
    "sc2": ("sbuf", [128, C], F32), "val2": ("sbuf", [128, C], F32), "bt2": ("sbuf", [128, C], BF),
    "fw": ("sbuf", [128, C], BF), "lrow2": ("sbuf", [128, C], F32),
    "d0": ("sbuf", [128, 7 * KW], F32), "d1": ("sbuf", [128, 7 * KW], F32), "f7": ("sbuf", [128, 7 * KW], F32),
    "sc": ("sbuf", [128, C], F32), "val": ("sbuf", [128, C], F32), "dd": ("sbuf", [128, C], BF),
    "tt": ("sbuf", [128, C], BF), "bt": ("sbuf", [128, C], BF), "app": ("sbuf", [128, C], BF),
    "vv": ("sbuf", [128, C], BF), "fv": ("sbuf", [128, C], BF), "fk": ("sbuf", [128, C], F32),
    "lrow": ("sbuf", [128, C], F32), "orow": ("sbuf", [128, C], F32), "oprow": ("sbuf", [128, C], F32),
    "oporow": ("sbuf", [128, C], F32), "ysb": ("sbuf", [128, C], F32),
    "ps_s": ("psum", [128, 512], F32), "ps_r": ("psum", [128, 2048], F32), "ps_p": ("psum", [128, 1536], F32),
}
SEMAPHORES = ["cv", "cs", "cp", "cg", "d_md", "d_mi", "d_x", "d_u", "d_v", "d_wc", "d_ws", "d_om", "d_oc", "d_y", "d_y2", "d_sc0",
              "d_sc1", "d_sc2", "d_sc3", "sent0", "sent", "h_list", "h_code", "h_scale",
              "a_list0", "a_list1", "a_list2", "a_code0", "a_code1", "a_code2", "a_scale0", "a_scale1", "a_scale2"]

A = AluOpType
COPY = ActivationFunctionType.Copy


def bits(engines):
    m = 0
    for e in engines:
        m |= 1 << e
    return m


def helpers(T, topo, src, dst):
    able = [c for c in topo.cores_of(src) if T.rank_of(c) is None and topo.may_write(c, dst)]
    near = [c for c in able if topo.die(c) == topo.die(src)]
    far = [c for c in able if topo.die(c) != topo.die(src)]
    return near[0], far[0]


def hand_on(g, core, T, topo, src, dst, half):
    rid, pid = topo.addr(dst, core)
    mask, n = topo.mask(core, dst), len(topo.engines(core, dst))
    nin = len(topo.engines(core, dst))
    total = 0
    if half == 0:
        g.wait_ge(T.sem.h_list, LIST_ENG)
        g.remote_dma(T.p0[:], T.rmd[:], T.sem.a_list0, T.sem.sent, pid, rid, mask)
        total += n
    g.wait_ge(T.sem.h_code, nin // 2)
    g.remote_dma(T.lq[:, half * H:half * H + H].bitcast(dt.uint8), T.rq[:].bitcast(dt.uint8), T.sem.a_code0, T.sem.sent, pid, rid, mask)
    g.wait_ge(T.sem.h_scale, nin // 2)
    g.remote_dma(T.ls[:, half * H:half * H + H], T.rs[:], T.sem.a_scale0, T.sem.sent, pid, rid, mask)
    g.wait_ge(T.sem.sent, total + 2 * n)


def rank_program(g, core, T, topo):
    rank = T.rank_of(core)
    if rank is None:
        for r, c in enumerate(T.cores):
            d = T.cores[r ^ STRIDE[0]]
            if core in topo.cores_of(c) and not topo.may_write(c, d):
                hs = helpers(T, topo, c, d)
                if core in hs:
                    hand_on(g, core, T, topo, c, d, hs.index(core))
        return

    eng = {"V": g.vector, "S": g.scalar, "P": g.tensor, "G": g, "Y": g.sync}
    csem = {"V": "cv", "S": "cs", "P": "cp", "G": "cg"}
    count, direct = {}, {}
    known = {q: {} for q in eng}
    wrote, readers = {}, {}

    def need(q, reads, writes, chain=False):
        deps = [wrote[k] for k in reads if k in wrote]
        for k in writes:
            if k in wrote and not chain:
                deps.append(wrote[k])
            deps += readers.get(k, [])
        top = {}
        for s, v, clk in deps:
            if v > known[q].get(s, 0) and v > top.get(s, (0, None))[0]:
                top[s] = (v, clk)
        for s in sorted(top):
            v, clk = top[s]
            if any(o != s and top[o][1].get(s, 0) >= v for o in top):
                continue
            eng[q].wait_ge(T.sem[s], v)
            direct[s] = max(direct.get(s, 0), v)
        for s in top:
            v, clk = top[s]
            known[q][s] = max(known[q].get(s, 0), v)
            for o in clk:
                known[q][o] = max(known[q].get(o, 0), clk[o])

    def done(q, s, n, reads, writes):
        count[s] = count.get(s, 0) + n
        ev = (s, count[s], dict(known[q]))
        for k in reads:
            readers.setdefault(k, []).append(ev)
        for k in writes:
            wrote[k] = ev
            readers[k] = []

    def op(q, call, reads, writes, chain=False):
        need(q, reads, writes, chain)
        call().then_inc(T.sem[csem[q]], 1)
        done(q, csem[q], 1, reads, writes)

    def dma(q, s, out, in_, reads, writes):
        need(q, reads, writes)
        eng[q].dma_start(out, in_).then_inc(T.sem[s], 16)
        done(q, s, 16, reads, writes)

    def lands(key, s, n):
        count[s] = n
        wrote[key] = (s, n, {})

    V, S, P = g.vector, g.scalar, g.tensor

    def ts(out, in0, s1, s2, op0, op1, reads, writes):
        if op1 is None:
            op("V", lambda: V.tensor_scalar(out, in0, s1, None, op0), reads, writes)
        else:
            op("V", lambda: V.tensor_scalar(out, in0, s1, s2, op0, op1), reads, writes)

    def cp(out, in_, reads, writes):
        op("V", lambda: V.tensor_copy(out, in_), reads, writes)

    def tt(out, in0, in1, alu, reads, writes):
        op("V", lambda: V.tensor_tensor(out, in0, in1, alu), reads, writes)

    def act(out, in_, scale, reads, writes):
        if scale is None:
            op("S", lambda: S.activation(out, in_, COPY), reads, writes)
        else:
            op("S", lambda: S.activation(out, in_, COPY, scale=scale), reads, writes)

    def quant(q, s, t, reads, writes):
        op("V", lambda: V.quantize_mx(q, s, t), reads, writes)

    def mm(out, lq, ls, rq, rs, start, stop, reads, bank):
        op("P", lambda: P.matmul_mx(out, lq, ls, rq, rs, start, stop), reads, [bank], chain=not start)

    def scan(out, d0, d1, reads, writes):
        op("V", lambda: V.tensor_tensor_scan(out, d0, d1, 0.0, A.mult, A.add), reads, writes)

    partner = [T.cores[rank ^ h] for h in STRIDE]
    relay = None if topo.may_write(core, partner[0]) else helpers(T, topo, core, partner[0])
    out_eng = topo.engines(relay[0] if relay else core, partner[0])
    ne = len(out_eng)

    def send(s_local, out, in_, s_remote, dst, reads, engines=out_eng):
        need("G", reads, [])
        rid, pid = topo.addr(dst, core)
        g.remote_dma(out, in_, T.sem[s_remote], T.sem[s_local], pid, rid, bits(engines))
        done("G", s_local, len(engines), [], [])

    def send_halves(outs, ins, s_remote, reads):
        need("G", reads, [])
        tr = []
        for i in range(2):
            rid, pid = topo.addr(relay[i], core)
            tr.append(RemoteDMATransfer(dst_ids=[DstId(rid=rid, pnc=pid)], dma_engine_mask=bits(out_eng[i::2]),
                                        remote_sem=T.sem[s_remote], src=ins[i], dst=outs[i]))
        g.remote_dma_fused(tr, local_sem=T.sem.sent0)
        done("G", "sent0", ne, [], [])

    for r in range(3):
        k = 2 if (r == 0 and relay) else 1
        lands("lq%d" % r, "a_code%d" % r, k * ne)
        lands("ls%d" % r, "a_scale%d" % r, k * ne)
    lands("p0", "a_list0", ne)
    lands("P1", "a_list1", ne)
    lands("P2", "a_list2", ne)

    def xq(r):
        return T.xq[:, r * C:(r + 1) * C], T.xs[:, r * C:(r + 1) * C]

    def own(r):
        return T.ml[:, 2 * KW * r:2 * KW * r + KW]

    def plist(r, low=0):
        if r == 0:
            return T.pl0[:, low * KW:low * KW + KW]
        return T.pl[:, 2 * KW * (r - 1) + low * KW:2 * KW * (r - 1) + low * KW + KW]

    def plane(t, b, w=C):
        return t[:, b * w:b * w + C]

    def bank(t, b):
        return t[:, 512 * b:512 * b + C]

    def ecol(b):
        return T.eq[:, 128 * b:128 * b + 128], T.es[:, 128 * b:128 * b + 128]

    pmf, pm1, thr, inv = [T.cols[:, i:i + 1] for i in range(4)]
    W7 = 7 * KW

    dma("Y", "d_md", T.md[:], T.m[:], [], ["md"])
    dma("S", "d_x", T.x0[:], T.x[:], [], ["x0"])
    dma("Y", "d_mi", T.mi[:], T.m[:], [], ["mi"])
    dma("Y", "d_u", T.ub[:], T.u[:], [], ["ub"])
    op("G", lambda: g.iota(T.di[:], [[-1, 128]], 0, 1), [], ["di"])
    op("G", lambda: g.iota(T.jrow[:], [[1, C]], 0, 0), [], ["jrow"])
    if relay:
        send("sent0", T.rmd[:], T.md[:], "h_list", relay[0], ["md"], out_eng[:LIST_ENG])
    else:
        send("sent0", T.p0[:], T.md[:], "a_list0", partner[0], ["md"])

    op("V", lambda: V.memset(T.eb[:], 0.0), [], ["eb%d" % b for b in range(4)])
    op("V", lambda: V.memset(T.d0[:], -1.0), [], ["d0c", "d0a", "d0b", "d0d"])
    ts(T.pmi[:], T.di[:, 0:1], 15, None, A.bitwise_and, None, ["di"], ["pmi"])
    for b in range(4):
        ts(T.eb[:, 512 * b + b:512 * b + 512:4], T.di[:], 0.0, 32.0, A.is_equal, A.mult, ["di"], ["eb%d" % b])
    ts(T.d0[:, 0:W7:7], T.di[:, 0:KW], 0.0, None, A.mult, None, ["di"], ["d0c"])
    cp(pmf, T.pmi[:], ["pmi"], ["pmf"])
    cp(T.uoff[:], T.jrow[:, 0:128:16], ["jrow"], ["uoff"])
    cp(own(0), T.mi[:], ["mi"], ["M0"])
    cp(T.jf[:], T.jrow[:], ["jrow"], ["jf"])
    quant(T.eq[:], T.es[:], T.eb[:], ["eb%d" % b for b in range(4)], ["eq"])

    def head(r):
        q, s = xq(r)
        if r == 0:
            quant(q, s, T.x0[:], ["x0"], ["xq0"])
        else:
            quant(q, s, T.xt[:], ["xt%d" % b for b in range(4)], ["xq%d" % r])
        if r == 3:
            return
        if r == 0 and relay:
            send_halves([T.rq[:].bitcast(dt.uint8)] * 2, [T.xq[:, i * H:i * H + H].bitcast(dt.uint8) for i in range(2)], "h_code", ["xq0"])
            send_halves([T.rs[:]] * 2, [T.xs[:, i * H:i * H + H] for i in range(2)], "h_scale", ["xq0"])
        else:
            sl = "sent0" if r == 0 else "sent"
            send(sl, T.lq[:, r * C:(r + 1) * C].bitcast(dt.uint8), q.bitcast(dt.uint8), "a_code%d" % r, partner[r], ["xq%d" % r])
            send(sl, T.ls[:, r * C:(r + 1) * C], s, "a_scale%d" % r, partner[r], ["xq%d" % r])

    quant(T.uq[:], T.us[:], T.ub[:], ["ub"], ["uq"])
    ts(pm1, T.pmi[:], 1.0, None, A.add, None, ["pmi"], ["pm1"])
    cp(T.uq2[:].bitcast(dt.uint32), T.uq[:].bitcast(dt.uint32).indirect(T.uoff[:]), ["uq", "uoff"], ["uq2"])
    cp(T.us2[:], T.us[:].indirect(T.uoff[:]), ["uq", "uoff"], ["us2"])
    head(0)
    wrote["sent0"] = ("sent0", count["sent0"], {})
    dma("Y", "d_wc", T.wq[:].bitcast(dt.uint8), T.wc[:], ["sent0"], ["wq"])
    dma("Y", "d_ws", T.wsc[:], T.ws[:], [], ["wsc"])
    dma("Y", "d_v", T.vb[:], T.v[:], [], ["vb"])

    ts(T.tm[:], T.jrow[:], 15, None, A.bitwise_and, None, ["jrow"], ["tm"])
    ts(T.jw[:], T.jrow[:, 0:C:16], pmf, None, A.add, None, ["jrow", "pmf"], ["jw"])
    ts(T.d1[:, 5:W7:7], T.jrow[:, 0:KW], 0.0, float(C), A.mult, A.add, ["jrow"], ["d1c"])
    ts(T.d1[:, 6:W7:7], T.jrow[:, 0:KW], 0.0, float(C), A.mult, A.add, ["jrow"], ["d1e"])
    for b in range(4):
        op("V", lambda: V.memset(T.fp[:, CZ * b + C:CZ * b + CZ], 0.0), [], ["fz%d" % b])
    ts(T.cj[:], T.jw[:], -1.0, float(C), A.mult, A.add, ["jw"], ["cj"])
    ts(T.ra[:], T.tm[:], pm1, 2.0 ** 60, A.is_equal, A.mult, ["tm", "pm1"], ["ra"])
    ts(T.rb[:], T.tm[:], pmf, None, A.not_equal, None, ["tm", "pmf"], ["rb"])
    ts(thr, T.pmi[:], -15.005, -100.0, A.add, A.mult, ["pmi"], ["thr"])
    ts(inv, T.pmi[:], 15.0, 2.0 ** -60, A.is_equal, A.add, ["pmi"], ["inv"])
    cp(T.d1[:, 1:W7:7], T.mi[:], ["mi"], ["d1o1"])
    cp(T.d1[:, 2:W7:7], T.mi[:], ["mi"], ["d1o2"])
    tt(T.rr[:], T.ra[:], T.rb[:], A.add, ["ra", "rb"], ["rr"])
    act(T.jt[:], T.jf[:], 2.0 ** -120, ["jf"], ["jt"])

    def o_row(r):
        act(T.orow[:], T.jf[:].indirect(own(r)), None, ["jf", "M%d" % r], ["orow"])

    def low_row(r):
        act(T.lrow[:], T.jt[:].indirect(plist(r, 1)), None, ["jt", "L0" if r == 0 else "P%d" % r], ["lrow"])

    def low_copy():
        act(T.lrow2[:], T.lrow[:], None, ["lrow"], ["lrow2"])

    def op_row(r):
        act(T.oprow[:], T.orow[:].indirect(plist(r)), None, ["orow", "P%d" % r], ["oprow"])

    def opo_row(r):
        act(T.oporow[:], T.oprow[:].indirect(own(r)), None, ["oprow", "M%d" % r], ["oporow"])

    o_row(0)

    for r in range(3):
        q, s = xq(r)
        XQ, M, PK = "xq%d" % r, "M%d" % r, "P%d" % r
        o, p = own(r), plist(r)
        mm(T.ps_s[:, 0:C], T.uq2[:], T.us2[:], q, s, True, True, ["uq2", "us2", XQ], "ps_s")
        mm(bank(T.ps_p, 2), T.uq2[:], T.us2[:], q, s, True, True, ["uq2", "us2", XQ], "ps_p2")
        for b in range(4):
            mm(bank(T.ps_r, b), *ecol(b), q, s, True, True, ["eq", XQ], "ps_r%d" % b)

        def s_op():
            act(T.sc[:], T.ps_s[:, 0:C], None, [], ["ps_s", "sc"])

        def s_copy():
            cp(T.sc2[:], bank(T.ps_p, 2), [], ["ps_p2", "sc2"])

        def fh_op(b):
            act(plane(T.fh, b), bank(T.ps_r, b), 2.0 ** -6, [], ["ps_r%d" % b, "fh%d" % b])

        def fo_op(b):
            act(plane(T.fo, b), plane(T.fh, b).indirect(o), None, ["fh%d" % b, M], ["fo%d" % b])

        def t_op(k):
            tt(T.tt[:], T.lrow[:].indirect(own(k)), T.lrow2[:], A.subtract, ["lrow", "lrow2", "M%d" % k], ["tt"])

        def val_op():
            tt(T.val[:], T.sc[:].indirect(p), T.sc2[:], A.max, ["sc", "sc2", PK], ["val"])

        def val_copy():
            cp(T.val2[:], T.val[:], ["val"], ["val2"])

        def d_op():
            tt(T.dd[:], T.val[:].indirect(o), T.val2[:], A.subtract, ["val", "val2", M], ["dd"])

        def beats_op():
            tt(T.bt[:], T.dd[:], T.tt[:], A.is_lt, ["dd", "tt"], ["bt"])

        def beats_copy():
            cp(T.bt2[:], T.bt[:], ["bt"], ["bt2"])

        def app_op():
            tt(T.app[:], T.bt[:].indirect(p), T.bt2[:], A.mult, ["bt", "bt2", PK], ["app"])

        def v_op():
            if r:
                act(T.vv[:], T.app[:].indirect(o), None, ["app", M], ["vv"])
            else:
                cp(T.vv[:], T.app[:].indirect(o), ["app", M], ["vv"])

        def scan_a():
            scan(T.fw[:], T.rr[:], T.app[:], ["rr", "app"], ["fw"])

        def scan_k():
            scan(T.fk[:], T.rr[:], T.oporow[:], ["rr", "oporow"], ["fk"])

        def opo_op():
            ts(T.d1[:, 0:W7:7], T.fk[:, 15:C:16], inv, None, A.mult, None, ["fk", "inv"], ["d1k"])

        def p_op(i):
            cp(T.d1[:, 3 + i:W7:7], p, [PK], ["d1p%d" % i])

        def o_op(i):
            cp(T.d1[:, i:W7:7], T.f7[:, 4:W7:7], ["f7"], ["d1o%d" % i])

        def scan_v():
            scan(T.fv[:], T.rr[:], T.vv[:], ["rr", "vv"], ["fv"])

        if r == 0:
            s_op(), s_copy(), fh_op(0), fh_op(1), fh_op(2), fh_op(3), fo_op(0), fo_op(1)
            cp(p, T.p0[:], ["p0"], ["P0"])
            tt(T.lowf[:], T.p0[:], T.jw[:], A.min, ["p0", "jw"], ["lowf"])
            cp(plist(0, 1), T.lowf[:], ["lowf"], ["L0"])
            low_row(0)
            low_copy()
            op_row(0)
            opo_row(0)
            fo_op(2), fo_op(3)
            val_op(), p_op(0), val_copy(), p_op(1), d_op(), t_op(0), beats_op(), beats_copy(), app_op()
            scan_k(), v_op(), scan_a(), scan_v(), opo_op()
        else:
            op_row(r), s_op(), fh_op(0), fh_op(1), fh_op(2), fh_op(3), fo_op(0), opo_row(r), fo_op(1)
            p_op(0), p_op(1), s_copy(), val_op(), o_op(1), val_copy(), o_op(2), d_op(), beats_op(), beats_copy(), app_op()
            v_op(), fo_op(2), fo_op(3), scan_a(), scan_k(), opo_op(), scan_v()
        fv, fw = T.fv[:, 15:C:16], T.fw[:, 15:C:16]
        ts(T.d0[:, 4:W7:7], fw, thr, -1.0, A.is_ge, A.add, ["fw", "thr"], ["d0b"])
        ts(T.d0[:, 6:W7:7], fw, thr, -1.0, A.is_ge, A.mult, ["fw", "thr"], ["d0d"])
        ts(T.d0[:, 2:W7:7], fv, thr, -1.0, A.is_ge, A.mult, ["fv", "thr"], ["d0a"])
        scan(T.f7[:], T.d0[:], T.d1[:], ["d0c", "d0a", "d0b", "d0d", "d1k", "d1o1", "d1o2", "d1p0", "d1p1", "d1c", "d1e"], ["f7"])
        MN, n = "M%d" % (r + 1), own(r + 1)
        cp(n, T.f7[:, 4:W7:7], ["f7"], [MN])

        def z_op(b):
            tt(T.zt[:, b:4 * C:4], plane(T.fh, b).indirect(n), plane(T.fo, b), A.add, ["fh%d" % b, "fo%d" % b, MN], ["zt%d" % b])

        tt(T.ajf[:], T.d0[:, 6:W7:7], T.cj[:], A.mult, ["d0d", "cj"], ["ajf"])
        if r < 2:
            tt(T.lowf[:], T.f7[:, 4:W7:7], T.jw[:], A.min, ["f7", "jw"], ["lowf"])
        z_op(0)
        ts(T.aj[:], T.ajf[:], float(C), None, A.add, None, ["ajf"], ["aj"])
        if r < 2:
            a = 2 * KW * (r + 1)
            cp(T.ml[:, a + KW:a + 2 * KW], T.lowf[:], ["lowf"], ["ML%d" % r])
            send("sent", T.pl[:, 2 * KW * r:2 * KW * (r + 1)], T.ml[:, a:a + 2 * KW], "a_list%d" % (r + 1), partner[r + 1], [MN, "ML%d" % r])
        z_op(1), z_op(2), z_op(3)
        cp(T.al[:], T.f7[:, 6:W7:7], ["f7"], ["al"])
        quant(T.zq[:], T.zs[:], T.zt[:], ["zt%d" % b for b in range(4)], ["zq"])

        lq, ls = T.lq[:, r * C:(r + 1) * C], T.ls[:, r * C:(r + 1) * C]

        def f_mm(b):
            mm(bank(T.ps_p, b % 3), *ecol(b), lq, ls, True, True, ["eq", "lq%d" % r, "ls%d" % r], "ps_p%d" % (b % 3))

        def f_copy(b):
            act(plane(T.fp, b, CZ), bank(T.ps_p, b % 3), 2.0 ** -6, [], ["ps_p%d" % (b % 3), "fp%d" % b])

        f_mm(0), f_mm(1), f_mm(2), f_copy(0), f_mm(3), f_copy(1), f_copy(2), f_copy(3)
        for b in range(4):
            act(plane(T.fa, b), T.fp[:, CZ * b:CZ * b + CZ].indirect(T.aj[:]), None, ["fp%d" % b, "fz%d" % b, "aj"], ["fa%d" % b])

        for b in range(4):
            mm(bank(T.ps_r, b), *ecol(b), q, s, True, False, ["eq", XQ], "ps_r%d" % b)
        for b in range(4):
            mm(bank(T.ps_r, b), T.wq[:, 128 * b:128 * b + 128], T.wsc[:, 128 * b:128 * b + 128], T.zq[:], T.zs[:], False, False,
               ["wq", "wsc", "zq"], "ps_r%d" % b)
        for b in range(4):
            tt(T.at[:, b:4 * C:4], T.fp[:, CZ * b:CZ * b + CZ].indirect(T.al[:]), plane(T.fa, b), A.add,
               ["fp%d" % b, "fz%d" % b, "fa%d" % b, "al"], ["at%d" % b])
        quant(T.aq[:], T.asc[:], T.at[:], ["at%d" % b for b in range(4)], ["aq"])
        for b in range(4):
            mm(bank(T.ps_r, b), *ecol(b), T.aq[:], T.asc[:], False, True, ["eq", "aq"], "ps_r%d" % b)

        if r < 2:
            low_row(r + 1), low_copy(), t_op(r + 1), o_row(r + 1)
        else:
            quant(T.vq[:], T.vs[:], T.vb[:], ["vb"], ["vq"])
            o_row(r + 1)
            dma("Y", "d_om", T.om[:], T.orow[0:128:16, :], ["orow"], [])
        for b in range(4):
            if b % 2 == 0:
                ts(T.xt[:, b:4 * C:4], bank(T.ps_r, b), 2.0 ** -5, None, A.mult, None, [], ["ps_r%d" % b, "xt%d" % b])
            else:
                act(T.xt[:, b:4 * C:4], bank(T.ps_r, b), 2.0 ** -5, [], ["ps_r%d" % b, "xt%d" % b])
        head(r + 1)

    q, s = xq(3)
    mm(T.ps_s[:, 0:H], T.vq[:], T.vs[:], T.xq[:, 3 * C:3 * C + H], T.xs[:, 3 * C:3 * C + H], True, True, ["vq", "xq3"], "ps_s")
    mm(T.ps_p[:, 0:H], T.vq[:], T.vs[:], T.xq[:, 3 * C + H:4 * C], T.xs[:, 3 * C + H:4 * C], True, True, ["vq", "xq3"], "ps_p0")
    dma("Y", "d_oc", T.oc[:], q.bitcast(dt.uint8), ["xq3"], [])
    for k in range(4):
        dma("YS"[k // 2], "d_sc%d" % k, T.osc[4 * k:4 * k + 4, :], T.xs[32 * k:32 * k + 4, 3 * C:4 * C], ["xq3"], [])
    cp(T.ysb[:, H:C], T.ps_p[:, 0:H], [], ["ps_p0", "ysb1"])
    act(T.ysb[:, 0:H], T.ps_s[:, 0:H], None, [], ["ps_s", "ysb0"])
    dma("S", "d_y", T.y[:, 0:H], T.ysb[:, 0:H], ["ysb0"], [])
    dma("Y", "d_y2", T.y[:, H:C], T.ysb[:, H:C], ["ysb1"], [])
    last = ["d_oc", "d_sc0", "d_sc1", "d_sc2", "d_sc3", "d_y", "d_y2"]
    for s in sorted(count, key=lambda s: (last.index(s) if s in last else -1, s)):
        if direct.get(s, 0) < count[s]:
            g.wait_ge(T.sem[s], count[s])
